import numpy as np
import ml_dtypes


def mxq(x, axis, fmt="e4m3"):
    dtype, down = {"e4m3": (ml_dtypes.float8_e4m3fn, 7), "e5m2": (ml_dtypes.float8_e5m2, 14)}[fmt]
    v = np.moveaxis(np.asarray(x, np.float32).astype(ml_dtypes.bfloat16).astype(np.float64), axis, -1)
    blocks = v.reshape(v.shape[:-1] + (-1, 32))
    amax = np.abs(blocks).max(-1, keepdims=True)
    byte = np.maximum(np.where(amax > 0, np.frexp(amax)[1] - 1 + 127, 0) - down, 1)
    scale = np.exp2(byte - 127.0)
    codes = (blocks / scale).astype(np.float32).astype(dtype).astype(np.float64)
    return np.moveaxis((codes * scale).reshape(v.shape), -1, axis)


WIDE = False


def mx_kscale(k):
    if not WIDE:
        return np.ones(k)
    levels = np.array([10, -10, 5, -5, 0])
    if k % 512:
        return np.exp2(np.random.permutation(np.resize(levels, k // 32))).repeat(32)
    a = np.empty((k // 512, 16))
    for p in range(k // 512):
        a[p, :8] = np.random.permutation(np.resize(levels, 8))
        for g in range(8):
            far = levels[np.abs(levels - a[p, g]) >= 10]
            a[p, g + 8] = far[np.random.randint(len(far))]
    return np.exp2(a.ravel()).repeat(32)


def f64(x):
    return np.asarray(x).astype(np.float64)


def striped(idx):
    return np.tile(idx.reshape(-1, 16).T, (8, 1)).astype(np.uint16)


def unstriped(offs):
    return offs[:16].T.reshape(-1).astype(np.int64)


def striped8(idx):
    return np.concatenate([x.reshape(-1, 16).T for x in idx]).astype(np.uint16)


def runs(offs, k):
    lists = np.stack([offs[16 * r : 16 * r + 16].T.reshape(-1) for r in range(8)]).astype(np.int64)
    return lists[np.arange(k) % 512 // 64]


def pack_weight(w):
    k, n = w.shape
    w = f64(np.asarray(w, np.float32).astype(ml_dtypes.bfloat16)).reshape(k // 32, 32, n)
    amax = np.abs(w).max(1)
    byte = np.clip(np.where(amax > 0, np.frexp(amax)[1] - 1 + 127 - 7, 1), 1, 254)
    scaled = (w * np.exp2(127.0 - byte)[:, None, :]).reshape(k, n).astype(np.float32)
    words = np.ascontiguousarray(scaled.reshape(k // 512, 128, 4, n).transpose(0, 1, 3, 2)).astype(ml_dtypes.float8_e4m3fn).view(np.uint8)
    return words, np.ascontiguousarray(byte.astype(np.uint8).reshape(k // 512, 16, n))


def unpack_weight(words, scales):
    g, p, n, _ = words.shape
    vals = np.ascontiguousarray(words).view(ml_dtypes.float8_e4m3fn).astype(np.float64) * np.repeat(np.exp2(scales.astype(np.float64) - 127.0), 8, axis=1)[..., None]
    return vals.transpose(0, 1, 3, 2).reshape(g * 512, n)


def sigmoid(v):
    return 1.0 / (1.0 + np.exp(-np.maximum(v, -700.0)))


K, T, S, H, W = 512, 2048, 512, 512, 256


def setup_inputs():
    n = np.random.standard_normal
    s = mx_kscale(K)[:, None]
    u = mx_kscale(S)
    packed_xT = pack_weight(n((K, T)) * s)
    perm = np.stack([np.random.permutation(S) for _ in range(8)])
    return {
        "x_words": packed_xT[0],
        "x_scales": packed_xT[1],
        "w1": (n((K, H)) / np.sqrt(K) / s).astype(np.float32),
        "ga": (np.random.uniform(0.5, 1.5, (H, 1)) * u[:, None]).astype(np.float32),
        "gb": (np.random.uniform(0.5, 1.5, (H, 1)) / u[:, None]).astype(np.float32),
        "offs": striped(np.random.permutation(T)[:S]),
        "n1": striped8(perm[:, :W]),
        "n2": striped8(perm[:, W:]),
        "n3": striped8(np.stack([np.random.permutation(S) for _ in range(8)])),
        "n4": striped8(np.stack([np.random.permutation(S) for _ in range(8)])),
        "n5": striped8(np.stack([np.random.permutation(S) for _ in range(8)])),
        "n6": striped8(np.stack([np.random.permutation(S) for _ in range(8)])),
        "n7": striped8(np.stack([np.random.permutation(S) for _ in range(8)])),
        "n8": striped8(np.stack([np.random.permutation(S) for _ in range(8)])),
        "n9": striped8(np.stack([np.random.permutation(S) for _ in range(8)])),
    }


def reference(x_words, x_scales, w1, ga, gb, offs, n1, n2, n3, n4, n5, n6, n7, n8, n9):
    xq = unpack_weight(x_words, x_scales)[:, unstriped(offs)]
    y = mxq(f64(w1), 0, "e4m3").T @ xq
    pa = y[np.arange(H)[:, None], runs(n1, H)]
    pb = y[np.arange(H)[:, None], runs(n2, H)]
    rb = np.maximum(pa, pb)
    ra = pa / (np.abs(pb) + 0.5)
    ds = np.zeros((H, S))
    ds[np.arange(H)[:, None], runs(n1, H)] = ra
    dt = ds.copy()
    dt[np.arange(H)[:, None], runs(n2, H)] = rb
    z = f64(ga) * dt
    z2 = f64(gb) * (0.75 * ((y[np.arange(H)[:, None], runs(n3, H)]) * (y[np.arange(H)[:, None], runs(n4, H)]) - ((y[np.arange(H)[:, None], runs(n5, H)]) * (y[np.arange(H)[:, None], runs(n6, H)]))))
    s = 0.0625 * ((mxq(z, 0, "e4m3").T @ mxq(z2, 0, "e4m3")))
    pa2 = s[np.arange(S)[:, None], runs(n7, S)]
    return pa2 + (sigmoid(s[np.arange(S)[:, None], runs(n8, S)])) * (s[np.arange(S)[:, None], runs(n9, S)] - pa2)

@@ -1,0 +1,186 @@
+from contextlib import ExitStack
+
+import concourse.mybir as mybir
+
+K, T, S, H, W = 512, 2048, 512, 512, 256
+P = 128
+PACK = 4
+HALF = S // 2
+COLS = HALF // 16
+
+F32 = mybir.dt.float32
+BF16 = mybir.dt.bfloat16
+I32 = mybir.dt.int32
+U32 = mybir.dt.uint32
+U16 = mybir.dt.uint16
+U8 = mybir.dt.uint8
+FP8X4 = mybir.dt.float8_e4m3fn_x4
+ALU = mybir.AluOpType
+ACT = mybir.ActivationFunctionType
+
+FLOPS = 2 * K * H * S + 2 * H * S * S
+
+
+def tile_picked_selfratiodetlerp_none_p_kernel(
+    tc, x_words, x_scales, w1, ga, gb, offs, n1, n2, n3, n4, n5, n6, n7, n8, n9, out
+):
+    nc = tc.nc
+    with ExitStack() as ctx:
+        held = ctx.enter_context(tc.tile_pool(name="held", bufs=1))
+        psum = ctx.enter_context(tc.psum_pool(name="psum", bufs=1))
+
+        def sb(shape, dtype, name):
+            return held.tile(shape, dtype, name=name, align_bytes=64)
+
+        def load_list(src, name):
+            lst = sb(list(src.shape), U16, name)
+            nc.sync.dma_start(lst[:], src)
+            return lst
+
+        def half_of(lst, h):
+            return lst[:, h * COLS : (h + 1) * COLS]
+
+        picks = load_list(offs, "picks")
+        w_raw = sb([P, PACK, H], F32, "w_raw")
+        nc.sync.dma_start(w_raw[:], w1.rearrange("(p j) c -> p j c", j=PACK))
+        x_table = sb([P, T], I32, "x_table")
+        nc.sync.dma_start(x_table[:], x_words[0].rearrange("p n r -> p (n r)").bitcast(I32))
+        xs_table = sb([P, T], U8, "xs_table")
+        nc.vector.memset(xs_table[:].bitcast(I32), 0)
+        for q in range(4):
+            nc.scalar.dma_start(
+                xs_table[32 * q : 32 * q + 4, :].bitcast(I32), x_scales[0, 4 * q : 4 * q + 4, :].bitcast(I32)
+            )
+        l1, l2 = load_list(n1, "l1"), load_list(n2, "l2")
+        l3, l4, l5, l6 = load_list(n3, "l3"), load_list(n4, "l4"), load_list(n5, "l5"), load_list(n6, "l6")
+        l7, l8, l9 = load_list(n7, "l7"), load_list(n8, "l8"), load_list(n9, "l9")
+        ga_sb = sb([P, PACK], F32, "ga_sb")
+        nc.sync.dma_start(ga_sb[:], ga.rearrange("(p t) o -> p (t o)", t=PACK))
+        gb_sb = sb([P, PACK], F32, "gb_sb")
+        nc.sync.dma_start(gb_sb[:], gb.rearrange("(p t) o -> p (t o)", t=PACK))
+        gb34 = sb([P, PACK], F32, "gb34")
+        nc.scalar.activation(gb34[:], gb_sb[:], ACT.Copy, scale=0.75)
+
+        xq_scales = sb([P, S], U8, "xq_scales")
+        nc.vector.tensor_copy(xq_scales[:], xs_table[:].indirect(picks[:]))
+        w_bf = sb([P, H * PACK], BF16, "w_bf")
+        w_dst = w_bf[:].rearrange("p (t m j) -> p m j t", t=PACK, j=PACK)
+        w_src = w_raw[:].rearrange("p j (m t) -> p m j t", t=PACK)
+        nc.vector.tensor_copy(w_dst[:, : P // 2], w_src[:, : P // 2])
+        nc.scalar.copy(w_dst[:, P // 2 :], w_src[:, P // 2 :])
+        w_codes = sb([P, H], U32, "w_codes")
+        w_scales = sb([P, H], U8, "w_scales")
+        nc.vector.quantize_mx(out=w_codes[:].bitcast(FP8X4), scales=w_scales[:], in_=w_bf[:])
+        xq_codes = sb([P, S], U32, "xq_codes")
+        y_ps = [psum.tile([P, S], F32, name=f"y_ps{t}") for t in range(PACK)]
+        for h in range(2):
+            cols = slice(h * HALF, (h + 1) * HALF)
+            nc.vector.tensor_copy(xq_codes[:, cols], x_table[:].bitcast(U32).indirect(half_of(picks, h)))
+            for t in range(PACK):
+                m = slice(t * P, (t + 1) * P)
+                nc.tensor.matmul_mx(
+                    out=y_ps[t][:, cols],
+                    lhsT=w_codes[:, m].bitcast(FP8X4),
+                    lhsT_scale=w_scales[:, m],
+                    rhs=xq_codes[:, cols].bitcast(FP8X4),
+                    rhs_scale=xq_scales[:, cols],
+                    start=True,
+                    stop=True,
+                )
+        y = [sb([P, S], F32, f"y{t}") for t in range(PACK)]
+        yb = [sb([P, S], F32, f"yb{t}") for t in range(PACK)]
+        for t in range(PACK):
+            nc.scalar.copy(y[t][:], y_ps[t][:])
+
+        pa = [sb([P, W], F32, f"pa{t}") for t in range(PACK)]
+        pb = [sb([P, W], F32, f"pb{t}") for t in range(PACK)]
+        rb = [sb([P, W], F32, f"rb{t}") for t in range(PACK)]
+        size = [sb([P, W], F32, f"size{t}") for t in range(PACK)]
+        root = [sb([P, W], F32, f"root{t}") for t in range(PACK)]
+        inv = [sb([P, W], F32, f"inv{t}") for t in range(PACK)]
+        dt = [sb([P, S], F32, f"dt{t}") for t in range(PACK)]
+        for t in range(PACK):
+            nc.vector.tensor_copy(pb[t][:], y[t][:].indirect(l2[:]))
+            nc.vector.tensor_copy(pa[t][:], y[t][:].indirect(l1[:]))
+            nc.scalar.activation(size[t][:], pb[t][:], ACT.Abs)
+            nc.scalar.activation(root[t][:], size[t][:], ACT.Abs_reciprocal_sqrt, bias=0.5)
+            nc.scalar.activation(inv[t][:], root[t][:], ACT.Square)
+        for t in range(PACK):
+            nc.vector.tensor_tensor(rb[t][:], pa[t][:], pb[t][:], ALU.max)
+        for t in range(PACK):
+            nc.scalar.activation(yb[t][:], y_ps[t][:], ACT.Copy, scale=gb34[:, t : t + 1])
+        for t in range(PACK):
+            nc.vector.tensor_copy(dt[t][:].indirect(l2[:]), rb[t][:])
+        for t in range(PACK):
+            nc.vector.tensor_tensor(dt[t][:].indirect(l1[:]), pa[t][:], inv[t][:], ALU.mult)
+        z_rows = sb([P, PACK, S], BF16, "z_rows")
+        for t in range(PACK):
+            nc.scalar.activation(
+                z_rows[:, t, :].rearrange("p (u m) -> p m u", u=PACK),
+                dt[t][:].rearrange("p (m u) -> p m u", u=PACK),
+                ACT.Copy,
+                scale=ga_sb[:, t : t + 1],
+            )
+        z_bf = sb([P, S * PACK], BF16, "z_bf")
+        nc.scalar.copy(
+            z_bf[:].rearrange("p (c i t) -> p c t i", i=4, t=PACK),
+            z_rows[:].rearrange("p t (c i) -> p c t i", i=4),
+        )
+        z_codes = sb([P, S], U32, "z_codes")
+        z_scales = sb([P, S], U8, "z_scales")
+
+        s_ps = [psum.tile([P, S], F32, name=f"s_ps{u}") for u in range(PACK)]
+        s = [sb([P, S], F32, f"s{u}") for u in range(PACK)]
+        for h in range(2):
+            cols = slice(h * HALF, (h + 1) * HALF)
+            first = sb([P, PACK, HALF], F32, f"first{h}")
+            third = sb([P, PACK, HALF], F32, f"third{h}")
+            plus = sb([P, PACK, HALF], F32, f"plus{h}")
+            minus = sb([P, PACK, HALF], F32, f"minus{h}")
+            for t in range(PACK):
+                nc.vector.tensor_copy(first[:, t, :], yb[t][:].indirect(half_of(l3, h)))
+                nc.vector.tensor_copy(third[:, t, :], yb[t][:].indirect(half_of(l5, h)))
+                nc.vector.tensor_tensor(plus[:, t, :], y[t][:].indirect(half_of(l4, h)), first[:, t, :], ALU.mult)
+                nc.vector.tensor_tensor(minus[:, t, :], y[t][:].indirect(half_of(l6, h)), third[:, t, :], ALU.mult)
+            z2_bf = sb([P, HALF * PACK], BF16, f"z2_bf{h}")
+            nc.vector.tensor_tensor(
+                z2_bf[:].rearrange("p (c i t) -> p c t i", i=4, t=PACK),
+                plus[:].rearrange("p t (c i) -> p c t i", i=4),
+                minus[:].rearrange("p t (c i) -> p c t i", i=4),
+                ALU.subtract,
+            )
+            if h == 0:
+                nc.vector.quantize_mx(out=z_codes[:].bitcast(FP8X4), scales=z_scales[:], in_=z_bf[:])
+            z2_codes = sb([P, HALF], U32, f"z2_codes{h}")
+            z2_scales = sb([P, HALF], U8, f"z2_scales{h}")
+            nc.vector.quantize_mx(out=z2_codes[:].bitcast(FP8X4), scales=z2_scales[:], in_=z2_bf[:])
+            for u in range(PACK):
+                m = slice(u * P, (u + 1) * P)
+                nc.tensor.matmul_mx(
+                    out=s_ps[u][:, cols],
+                    lhsT=z_codes[:, m].bitcast(FP8X4),
+                    lhsT_scale=z_scales[:, m],
+                    rhs=z2_codes[:].bitcast(FP8X4),
+                    rhs_scale=z2_scales[:],
+                    start=True,
+                    stop=True,
+                )
+                nc.scalar.activation(s[u][:, cols], s_ps[u][:, cols], ACT.Copy, scale=0.0625)
+
+        out_rows = out.rearrange("(p u) j -> p u j", u=PACK)
+        for u in range(PACK):
+            gate = sb([P, S], F32, f"gate{u}")
+            rest = sb([P, S], F32, f"rest{u}")
+            kept = sb([P, S], F32, f"kept{u}")
+            taken = sb([P, S], F32, f"taken{u}")
+            blend = sb([P, S], F32, f"blend{u}")
+            for h in range(2):
+                cols = slice(h * HALF, (h + 1) * HALF)
+                nc.scalar.activation(gate[:, cols], s[u][:].indirect(half_of(l8, h)), ACT.Sigmoid)
+                nc.scalar.activation(rest[:, cols], gate[:, cols], ACT.Identity, scale=-1.0, bias=1.0)
+            for h in range(2):
+                cols = slice(h * HALF, (h + 1) * HALF)
+                nc.vector.tensor_tensor(taken[:, cols], s[u][:].indirect(half_of(l9, h)), gate[:, cols], ALU.mult)
+                nc.vector.tensor_tensor(kept[:, cols], s[u][:].indirect(half_of(l7, h)), rest[:, cols], ALU.mult)
+            nc.vector.tensor_tensor(blend[:], taken[:], kept[:], ALU.add)
+            nc.sync.dma_start(out_rows[:, u, :], blend[:])

@@ -1,6 +1,7 @@
 from contextlib import ExitStack
 
 import concourse.mybir as mybir
+from concourse.masks import make_identity
 
 K, T, S, H, W = 512, 2048, 512, 512, 256
 P = 128
@@ -40,26 +41,31 @@ def tile_picked_selfratiodetlerp_none_p_kernel(
         def half_of(lst, h):
             return lst[:, h * COLS : (h + 1) * COLS]
 
+        xs_table = sb([P, T], U8, "xs_table")
+        nc.gpsimd.memset(xs_table[:].bitcast(I32), 0)
         picks = load_list(offs, "picks")
         w_raw = sb([P, PACK, H], F32, "w_raw")
         nc.sync.dma_start(w_raw[:], w1.rearrange("(p j) c -> p j c", j=PACK))
-        x_table = sb([P, T], I32, "x_table")
-        nc.sync.dma_start(x_table[:], x_words[0].rearrange("p n r -> p (n r)").bitcast(I32))
-        xs_table = sb([P, T], U8, "xs_table")
-        nc.vector.memset(xs_table[:].bitcast(I32), 0)
         for q in range(4):
-            nc.scalar.dma_start(
+            nc.sync.dma_start(
                 xs_table[32 * q : 32 * q + 4, :].bitcast(I32), x_scales[0, 4 * q : 4 * q + 4, :].bitcast(I32)
             )
-        l1, l2 = load_list(n1, "l1"), load_list(n2, "l2")
-        l3, l4, l5, l6 = load_list(n3, "l3"), load_list(n4, "l4"), load_list(n5, "l5"), load_list(n6, "l6")
-        l7, l8, l9 = load_list(n7, "l7"), load_list(n8, "l8"), load_list(n9, "l9")
-        ga_sb = sb([P, PACK], F32, "ga_sb")
-        nc.sync.dma_start(ga_sb[:], ga.rearrange("(p t) o -> p (t o)", t=PACK))
+        x_table = sb([P, T], I32, "x_table")
+        nc.sync.dma_start(x_table[:], x_words[0].rearrange("p n r -> p (n r)").bitcast(I32))
+        l2, l1 = load_list(n2, "l2"), load_list(n1, "l1")
         gb_sb = sb([P, PACK], F32, "gb_sb")
         nc.sync.dma_start(gb_sb[:], gb.rearrange("(p t) o -> p (t o)", t=PACK))
-        gb34 = sb([P, PACK], F32, "gb34")
-        nc.scalar.activation(gb34[:], gb_sb[:], ACT.Copy, scale=0.75)
+        l3, l5, l4, l6 = load_list(n3, "l3"), load_list(n5, "l5"), load_list(n4, "l4"), load_list(n6, "l6")
+        ga_sb = sb([P, PACK], F32, "ga_sb")
+        nc.sync.dma_start(ga_sb[:], ga.rearrange("(p t) o -> p (t o)", t=PACK))
+        l8, l9, l7 = load_list(n8, "l8"), load_list(n9, "l9"), load_list(n7, "l7")
+
+        s = [sb([P, 2 * S], F32, f"s{u}") for u in range(PACK)]
+        for u in range(PACK):
+            nc.gpsimd.memset(s[u][:, S:], 0.0)
+
+        ident = sb([P, P], F32, "ident")
+        make_identity(nc, ident[:])
 
         xq_scales = sb([P, S], U8, "xq_scales")
         nc.vector.tensor_copy(xq_scales[:], xs_table[:].indirect(picks[:]))
@@ -72,14 +78,24 @@ def tile_picked_selfratiodetlerp_none_p_kernel(
         w_scales = sb([P, H], U8, "w_scales")
         nc.vector.quantize_mx(out=w_codes[:].bitcast(FP8X4), scales=w_scales[:], in_=w_bf[:])
         xq_codes = sb([P, S], U32, "xq_codes")
-        y_ps = [psum.tile([P, S], F32, name=f"y_ps{t}") for t in range(PACK)]
+        def bank(b, name):
+            return psum.tile([P, S], F32, name=name, tag=f"bank{b}")
+
         for h in range(2):
             cols = slice(h * HALF, (h + 1) * HALF)
             nc.vector.tensor_copy(xq_codes[:, cols], x_table[:].bitcast(U32).indirect(half_of(picks, h)))
-            for t in range(PACK):
-                m = slice(t * P, (t + 1) * P)
+        y_ps = [bank(t, f"y_ps{t}") for t in range(PACK)]
+        y_hi = bank(PACK, "y_hi")
+
+        def y_sum(t, h):
+            return y_hi[:, :HALF] if (t, h) == (0, 1) else y_ps[t][:, h * HALF : (h + 1) * HALF]
+
+        for t in range(PACK):
+            m = slice(t * P, (t + 1) * P)
+            for h in range(2):
+                cols = slice(h * HALF, (h + 1) * HALF)
                 nc.tensor.matmul_mx(
-                    out=y_ps[t][:, cols],
+                    out=y_sum(t, h),
                     lhsT=w_codes[:, m].bitcast(FP8X4),
                     lhsT_scale=w_scales[:, m],
                     rhs=xq_codes[:, cols].bitcast(FP8X4),
@@ -89,7 +105,10 @@ def tile_picked_selfratiodetlerp_none_p_kernel(
                 )
         y = [sb([P, S], F32, f"y{t}") for t in range(PACK)]
         yb = [sb([P, S], F32, f"yb{t}") for t in range(PACK)]
-        for t in range(PACK):
+        yn = [sb([P, S], F32, f"yn{t}") for t in range(PACK)]
+        nc.scalar.copy(y[0][:, :HALF], y_sum(0, 0))
+        nc.vector.tensor_copy(y[0][:, HALF:], y_sum(0, 1))
+        for t in range(1, PACK):
             nc.scalar.copy(y[t][:], y_ps[t][:])
 
         pa = [sb([P, W], F32, f"pa{t}") for t in range(PACK)]
@@ -107,8 +126,11 @@ def tile_picked_selfratiodetlerp_none_p_kernel(
             nc.scalar.activation(inv[t][:], root[t][:], ACT.Square)
         for t in range(PACK):
             nc.vector.tensor_tensor(rb[t][:], pa[t][:], pb[t][:], ALU.max)
+        gb34 = sb([P, PACK], F32, "gb34")
+        nc.scalar.activation(gb34[:], gb_sb[:], ACT.Copy, scale=0.75)
         for t in range(PACK):
-            nc.scalar.activation(yb[t][:], y_ps[t][:], ACT.Copy, scale=gb34[:, t : t + 1])
+            nc.scalar.activation(yb[t][:], y[t][:], ACT.Copy, scale=gb34[:, t : t + 1])
+            nc.scalar.activation(yn[t][:], yb[t][:], ACT.Copy, scale=-1.0)
         for t in range(PACK):
             nc.vector.tensor_copy(dt[t][:].indirect(l2[:]), rb[t][:])
         for t in range(PACK):
@@ -121,66 +143,130 @@ def tile_picked_selfratiodetlerp_none_p_kernel(
                 ACT.Copy,
                 scale=ga_sb[:, t : t + 1],
             )
-        z_bf = sb([P, S * PACK], BF16, "z_bf")
+        z_bf = held.tile([P, S * PACK], BF16, name="z_bf", tag="z_bf", align_bytes=64)
         nc.scalar.copy(
             z_bf[:].rearrange("p (c i t) -> p c t i", i=4, t=PACK),
             z_rows[:].rearrange("p t (c i) -> p c t i", i=4),
         )
         z_codes = sb([P, S], U32, "z_codes")
         z_scales = sb([P, S], U8, "z_scales")
+        warm = sb([P, 1], F32, "warm")
+        nc.scalar.activation(warm[:], inv[PACK - 1][:, 0:1], ACT.Sigmoid)
 
-        s_ps = [psum.tile([P, S], F32, name=f"s_ps{u}") for u in range(PACK)]
-        s = [sb([P, S], F32, f"s{u}") for u in range(PACK)]
-        for h in range(2):
-            cols = slice(h * HALF, (h + 1) * HALF)
-            first = sb([P, PACK, HALF], F32, f"first{h}")
-            third = sb([P, PACK, HALF], F32, f"third{h}")
-            plus = sb([P, PACK, HALF], F32, f"plus{h}")
-            minus = sb([P, PACK, HALF], F32, f"minus{h}")
-            for t in range(PACK):
-                nc.vector.tensor_copy(first[:, t, :], yb[t][:].indirect(half_of(l3, h)))
-                nc.vector.tensor_copy(third[:, t, :], yb[t][:].indirect(half_of(l5, h)))
-                nc.vector.tensor_tensor(plus[:, t, :], y[t][:].indirect(half_of(l4, h)), first[:, t, :], ALU.mult)
-                nc.vector.tensor_tensor(minus[:, t, :], y[t][:].indirect(half_of(l6, h)), third[:, t, :], ALU.mult)
-            z2_bf = sb([P, HALF * PACK], BF16, f"z2_bf{h}")
-            nc.vector.tensor_tensor(
-                z2_bf[:].rearrange("p (c i t) -> p c t i", i=4, t=PACK),
-                plus[:].rearrange("p t (c i) -> p c t i", i=4),
-                minus[:].rearrange("p t (c i) -> p c t i", i=4),
-                ALU.subtract,
+        z2_codes = sb([P, S], U32, "z2_codes")
+        z2_scales = sb([P, S], U8, "z2_scales")
+        s_ps = [bank(PACK + u, f"s_ps{u}") for u in range(PACK)]
+
+        def products(t, c0, c1, first, third, plus, minus):
+            lc = slice(c0 // 16, c1 // 16)
+            nc.vector.tensor_copy(first, yb[t][:].indirect(l3[:, lc]))
+            nc.vector.tensor_copy(third, yn[t][:].indirect(l5[:, lc]))
+            nc.vector.tensor_tensor(plus, y[t][:].indirect(l4[:, lc]), first, ALU.mult)
+            nc.vector.tensor_tensor(minus, y[t][:].indirect(l6[:, lc]), third, ALU.mult)
+
+        def quantise_z2(src, c0, a, b):
+            nc.vector.quantize_mx(
+                out=z2_codes[:, a:b].bitcast(FP8X4),
+                scales=z2_scales[:, a:b],
+                in_=src[:, (a - c0) * PACK : (b - c0) * PACK],
             )
-            if h == 0:
-                nc.vector.quantize_mx(out=z_codes[:].bitcast(FP8X4), scales=z_scales[:], in_=z_bf[:])
-            z2_codes = sb([P, HALF], U32, f"z2_codes{h}")
-            z2_scales = sb([P, HALF], U8, f"z2_scales{h}")
-            nc.vector.quantize_mx(out=z2_codes[:].bitcast(FP8X4), scales=z2_scales[:], in_=z2_bf[:])
-            for u in range(PACK):
-                m = slice(u * P, (u + 1) * P)
-                nc.tensor.matmul_mx(
-                    out=s_ps[u][:, cols],
-                    lhsT=z_codes[:, m].bitcast(FP8X4),
-                    lhsT_scale=z_scales[:, m],
-                    rhs=z2_codes[:].bitcast(FP8X4),
-                    rhs_scale=z2_scales[:],
-                    start=True,
-                    stop=True,
-                )
-                nc.scalar.activation(s[u][:, cols], s_ps[u][:, cols], ACT.Copy, scale=0.0625)
+
+        def second_product(u, a, b):
+            m = slice(u * P, (u + 1) * P)
+            nc.tensor.matmul_mx(
+                out=s_ps[u][:, a:b],
+                lhsT=z_codes[:, m].bitcast(FP8X4),
+                lhsT_scale=z_scales[:, m],
+                rhs=z2_codes[:, a:b].bitcast(FP8X4),
+                rhs_scale=z2_scales[:, a:b],
+                start=True,
+                stop=True,
+            )
+
+        A = 384
+        first = sb([P, PACK, A], F32, "first")
+        third = sb([P, PACK, A], F32, "third")
+        plus = sb([P, PACK, A], F32, "plus")
+        minus = sb([P, PACK, A], F32, "minus")
+        turned = [bank(b, f"turned{b}") for b in range(A // P)]
+        for t in range(PACK):
+            products(t, 0, A, first[:, t, :], third[:, t, :], plus[:, t, :], minus[:, t, :])
+            for b in range(A // P):
+                for i, term in enumerate((plus, minus)):
+                    nc.tensor.matmul(
+                        turned[b][:, t * P : (t + 1) * P],
+                        term[:, t, b * P : (b + 1) * P],
+                        ident[:],
+                        start=(i == 0),
+                        stop=(i == 1),
+                        is_transpose=True,
+                    )
+        z2_bf = held.tile([P, A * PACK], BF16, name="z2_bf", tag="z2_bf", align_bytes=64)
+        for b in range(A // P):
+            z2_t = sb([P, S], BF16, f"z2_t{b}")
+            nc.scalar.copy(
+                z2_t[:].rearrange("j (v p e) -> j v p e", v=2, e=2),
+                turned[b][:].rearrange("j (v e p) -> j v p e", v=2, e=2),
+            )
+            back = bank(3 if b < 2 else 0, f"back{b}")
+            for v in range(2):
+                nc.tensor.transpose(back[:, v * P : (v + 1) * P], z2_t[:].bitcast(F32)[:, v * P : (v + 1) * P], ident[:])
+            nc.scalar.copy(
+                z2_bf[:].bitcast(F32)[:, 2 * b * P : 2 * (b + 1) * P].rearrange("p (j v) -> p j v", v=2),
+                back[:, : 2 * P].rearrange("p (v j) -> p j v", v=2),
+            )
+        nc.vector.quantize_mx(out=z_codes[:].bitcast(FP8X4), scales=z_scales[:], in_=z_bf[:])
+        for a, b in ((0, 256), (256, A)):
+            quantise_z2(z2_bf, 0, a, b)
+        for u in range(PACK):
+            for a, b in ((0, 256), (256, A)):
+                second_product(u, a, b)
+            nc.scalar.activation(s[u][:, :A], s_ps[u][:, :A], ACT.Copy, scale=0.0625)
+
+        n = S - A
+        third2 = sb([P, PACK, n], F32, "third2")
+        plus2 = sb([P, PACK, n], F32, "plus2")
+        minus2 = sb([P, PACK, n], F32, "minus2")
+        for t in range(PACK):
+            tag = {0: "z_bf", PACK - 1: "z2_bf"}.get(t, f"first2{t}")
+            first2 = held.tile([P, n], F32, name=f"first2{t}", tag=tag, align_bytes=64)
+            products(t, A, S, first2[:], third2[:, t, :], plus2[:, t, :], minus2[:, t, :])
+        z2_bf2 = sb([P, n * PACK], BF16, "z2_bf2")
+        nc.vector.tensor_tensor(
+            z2_bf2[:].rearrange("p (c i t) -> p c t i", i=4, t=PACK),
+            plus2[:].rearrange("p t (c i) -> p c t i", i=4),
+            minus2[:].rearrange("p t (c i) -> p c t i", i=4),
+            ALU.add,
+        )
+        quantise_z2(z2_bf2, A, A, S)
+        for u in range(PACK):
+            second_product(u, A, S)
 
         out_rows = out.rearrange("(p u) j -> p u j", u=PACK)
+        gate = [sb([P, S], F32, f"gate{u}") for u in range(PACK)]
+        rest = [sb([P, S], F32, f"rest{u}") for u in range(PACK)]
+        kept = [sb([P, S], F32, f"kept{u}") for u in range(PACK)]
+        taken = [sb([P, S], F32, f"taken{u}") for u in range(PACK)]
+        last = sb([P, S], F32, "last")
         for u in range(PACK):
-            gate = sb([P, S], F32, f"gate{u}")
-            rest = sb([P, S], F32, f"rest{u}")
-            kept = sb([P, S], F32, f"kept{u}")
-            taken = sb([P, S], F32, f"taken{u}")
-            blend = sb([P, S], F32, f"blend{u}")
-            for h in range(2):
-                cols = slice(h * HALF, (h + 1) * HALF)
-                nc.scalar.activation(gate[:, cols], s[u][:].indirect(half_of(l8, h)), ACT.Sigmoid)
-                nc.scalar.activation(rest[:, cols], gate[:, cols], ACT.Identity, scale=-1.0, bias=1.0)
-            for h in range(2):
-                cols = slice(h * HALF, (h + 1) * HALF)
-                nc.vector.tensor_tensor(taken[:, cols], s[u][:].indirect(half_of(l9, h)), gate[:, cols], ALU.mult)
-                nc.vector.tensor_tensor(kept[:, cols], s[u][:].indirect(half_of(l7, h)), rest[:, cols], ALU.mult)
-            nc.vector.tensor_tensor(blend[:], taken[:], kept[:], ALU.add)
-            nc.sync.dma_start(out_rows[:, u, :], blend[:])
+            nc.scalar.activation(s[u][:, 384:512], s_ps[u][:, 384:512], ACT.Copy, scale=0.0625)
+            parts = ((0, 256), (256, 512)) if u in (0, PACK - 1) else ((0, 512),)
+            for a, b in parts:
+                nc.scalar.activation(gate[u][:, a:b], s[u][:].indirect(l8[:, a // 16 : b // 16]), ACT.Sigmoid)
+                nc.scalar.activation(rest[u][:, a:b], gate[u][:, a:b], ACT.Identity, scale=-1.0, bias=1.0)
+            for a, b in parts:
+                nc.vector.tensor_tensor(
+                    taken[u][:, a:b], s[u][:].indirect(l9[:, a // 16 : b // 16]), gate[u][:, a:b], ALU.mult
+                )
+                if u > 0 and b == S:
+                    nc.vector.tensor_tensor(gate[u][:], taken[u - 1][:], kept[u - 1][:], ALU.add)
+                    nc.sync.dma_start(out_rows[:, u - 1, :], gate[u][:])
+                if u == PACK - 1 and a > 0:
+                    nc.vector.tensor_tensor(last[:, :a], taken[u][:, :a], kept[u][:, :a], ALU.add)
+                    nc.sync.dma_start(out_rows[:, u, :a], last[:, :a])
+                nc.vector.tensor_tensor(
+                    kept[u][:, a:b], s[u][:].indirect(l7[:, a // 16 : b // 16]), rest[u][:, a:b], ALU.mult
+                )
+        u = PACK - 1
+        nc.vector.tensor_tensor(last[:, HALF:], taken[u][:, HALF:], kept[u][:, HALF:], ALU.add)
+        nc.sync.dma_start(out_rows[:, u, HALF:], last[:, HALF:])

@@ -7,7 +7,6 @@ K, T, S, H, W = 512, 2048, 512, 512, 256
 P = 128
 PACK = 4
 HALF = S // 2
-COLS = HALF // 16
 
 F32 = mybir.dt.float32
 BF16 = mybir.dt.bfloat16
@@ -30,16 +29,33 @@ def tile_picked_selfratiodetlerp_none_p_kernel(
         held = ctx.enter_context(tc.tile_pool(name="held", bufs=1))
         psum = ctx.enter_context(tc.psum_pool(name="psum", bufs=1))
 
-        def sb(shape, dtype, name):
-            return held.tile(shape, dtype, name=name, align_bytes=64)
+        def sb(shape, dtype, name, tag=None):
+            return held.tile(shape, dtype, name=name, tag=tag or name, align_bytes=64)
+
+        def bank(b, name):
+            return psum.tile([P, S], F32, name=name, tag=f"bank{b}")
 
         def load_list(src, name):
             lst = sb(list(src.shape), U16, name)
             nc.sync.dma_start(lst[:], src)
             return lst
 
-        def half_of(lst, h):
-            return lst[:, h * COLS : (h + 1) * COLS]
+        def entries(lst, a, b):
+            return lst[:, a // 16 : b // 16]
+
+        def quantise(codes, scales, values):
+            nc.vector.quantize_mx(out=codes.bitcast(FP8X4), scales=scales, in_=values)
+
+        def product(acc, left, left_scales, right, right_scales):
+            nc.tensor.matmul_mx(
+                out=acc,
+                lhsT=left.bitcast(FP8X4),
+                lhsT_scale=left_scales,
+                rhs=right.bitcast(FP8X4),
+                rhs_scale=right_scales,
+                start=True,
+                stop=True,
+            )
 
         xs_table = sb([P, T], U8, "xs_table")
         nc.gpsimd.memset(xs_table[:].bitcast(I32), 0)
@@ -52,20 +68,26 @@ def tile_picked_selfratiodetlerp_none_p_kernel(
             )
         x_table = sb([P, T], I32, "x_table")
         nc.sync.dma_start(x_table[:], x_words[0].rearrange("p n r -> p (n r)").bitcast(I32))
-        l2, l1 = load_list(n2, "l2"), load_list(n1, "l1")
+        l1, l2 = load_list(n1, "l1"), load_list(n2, "l2")
         gb_sb = sb([P, PACK], F32, "gb_sb")
         nc.sync.dma_start(gb_sb[:], gb.rearrange("(p t) o -> p (t o)", t=PACK))
         l3, l5, l4, l6 = load_list(n3, "l3"), load_list(n5, "l5"), load_list(n4, "l4"), load_list(n6, "l6")
         ga_sb = sb([P, PACK], F32, "ga_sb")
         nc.sync.dma_start(ga_sb[:], ga.rearrange("(p t) o -> p (t o)", t=PACK))
-        l8, l9, l7 = load_list(n8, "l8"), load_list(n9, "l9"), load_list(n7, "l7")
+        l7, l9, l8 = load_list(n7, "l7"), load_list(n9, "l9"), load_list(n8, "l8")
 
-        s = [sb([P, 2 * S], F32, f"s{u}") for u in range(PACK)]
-        for u in range(PACK):
-            nc.gpsimd.memset(s[u][:, S:], 0.0)
-
+        rows = [sb([P, 2 * S], F32, f"rows{t}") for t in range(PACK)]
+        yb = [sb([P, 2 * S], F32, f"yb{t}") for t in range(PACK)]
+        for t in range(PACK):
+            nc.vector.memset(rows[t][:, S:], 0.0)
+        warm_ln = sb([P, 1], F32, "warm_ln")
+        nc.scalar.activation(warm_ln[:], rows[0][:, S : S + 1], ACT.Ln, bias=0.5)
         ident = sb([P, P], F32, "ident")
         make_identity(nc, ident[:])
+        for t in range(PACK):
+            nc.gpsimd.memset(yb[t][:, S:], 0.0)
+        gb34 = sb([P, PACK], F32, "gb34")
+        nc.gpsimd.tensor_scalar(gb34[:], gb_sb[:], 0.75, 0.0, ALU.mult, ALU.add)
 
         xq_scales = sb([P, S], U8, "xq_scales")
         nc.vector.tensor_copy(xq_scales[:], xs_table[:].indirect(picks[:]))
@@ -74,125 +96,67 @@ def tile_picked_selfratiodetlerp_none_p_kernel(
         w_src = w_raw[:].rearrange("p j (m t) -> p m j t", t=PACK)
         nc.vector.tensor_copy(w_dst[:, : P // 2], w_src[:, : P // 2])
         nc.scalar.copy(w_dst[:, P // 2 :], w_src[:, P // 2 :])
-        w_codes = sb([P, H], U32, "w_codes")
+        w_codes = sb([P, H], U32, "w_codes", tag="xs_table")
         w_scales = sb([P, H], U8, "w_scales")
-        nc.vector.quantize_mx(out=w_codes[:].bitcast(FP8X4), scales=w_scales[:], in_=w_bf[:])
-        xq_codes = sb([P, S], U32, "xq_codes")
-        def bank(b, name):
-            return psum.tile([P, S], F32, name=name, tag=f"bank{b}")
-
-        for h in range(2):
-            cols = slice(h * HALF, (h + 1) * HALF)
-            nc.vector.tensor_copy(xq_codes[:, cols], x_table[:].bitcast(U32).indirect(half_of(picks, h)))
+        quantise(w_codes[:], w_scales[:], w_bf[:])
+        xq_codes = sb([P, S], U32, "xq_codes", tag="w_bf")
+        for a in (0, HALF):
+            nc.vector.tensor_copy(
+                xq_codes[:, a : a + HALF], x_table[:].bitcast(U32).indirect(entries(picks, a, a + HALF))
+            )
         y_ps = [bank(t, f"y_ps{t}") for t in range(PACK)]
-        y_hi = bank(PACK, "y_hi")
-
-        def y_sum(t, h):
-            return y_hi[:, :HALF] if (t, h) == (0, 1) else y_ps[t][:, h * HALF : (h + 1) * HALF]
-
+        y_ps_late = bank(PACK, "y_ps_late")
         for t in range(PACK):
             m = slice(t * P, (t + 1) * P)
-            for h in range(2):
-                cols = slice(h * HALF, (h + 1) * HALF)
-                nc.tensor.matmul_mx(
-                    out=y_sum(t, h),
-                    lhsT=w_codes[:, m].bitcast(FP8X4),
-                    lhsT_scale=w_scales[:, m],
-                    rhs=xq_codes[:, cols].bitcast(FP8X4),
-                    rhs_scale=xq_scales[:, cols],
-                    start=True,
-                    stop=True,
-                )
-        y = [sb([P, S], F32, f"y{t}") for t in range(PACK)]
-        yb = [sb([P, S], F32, f"yb{t}") for t in range(PACK)]
-        yn = [sb([P, S], F32, f"yn{t}") for t in range(PACK)]
-        nc.scalar.copy(y[0][:, :HALF], y_sum(0, 0))
-        nc.vector.tensor_copy(y[0][:, HALF:], y_sum(0, 1))
+            for a in (0, HALF):
+                cols = slice(a, a + HALF)
+                acc = y_ps_late if (t, a) == (0, HALF) else y_ps[t]
+                product(acc[:, cols], w_codes[:, m], w_scales[:, m], xq_codes[:, cols], xq_scales[:, cols])
+        nc.scalar.copy(rows[0][:, :HALF], y_ps[0][:, :HALF])
+        nc.vector.tensor_copy(rows[0][:, HALF:S], y_ps_late[:, HALF:])
         for t in range(1, PACK):
-            nc.scalar.copy(y[t][:], y_ps[t][:])
+            nc.scalar.copy(rows[t][:, :S], y_ps[t][:])
 
-        pa = [sb([P, W], F32, f"pa{t}") for t in range(PACK)]
-        pb = [sb([P, W], F32, f"pb{t}") for t in range(PACK)]
-        rb = [sb([P, W], F32, f"rb{t}") for t in range(PACK)]
-        size = [sb([P, W], F32, f"size{t}") for t in range(PACK)]
-        root = [sb([P, W], F32, f"root{t}") for t in range(PACK)]
-        inv = [sb([P, W], F32, f"inv{t}") for t in range(PACK)]
+        pa = sb([P, PACK, W], F32, "pa")
+        gap = sb([P, PACK, W], F32, "gap")
+        lift = sb([P, PACK, W], F32, "lift")
         dt = [sb([P, S], F32, f"dt{t}") for t in range(PACK)]
+        for t0 in range(0, PACK, 2):
+            pair = (t0, t0 + 1)
+            for t in pair:
+                nc.vector.tensor_copy(pa[:, t, :], rows[t][:].indirect(l1[:]))
+            for t in pair:
+                nc.vector.tensor_tensor(gap[:, t, :], rows[t][:].indirect(l2[:]), pa[:, t, :], ALU.subtract)
+            for t in pair:
+                nc.scalar.activation(yb[t][:, :S], rows[t][:, :S], ACT.Copy, scale=gb34[:, t : t + 1])
+            nc.scalar.activation(lift[:, t0 : t0 + 2, :], gap[:, t0 : t0 + 2, :], ACT.Relu)
         for t in range(PACK):
-            nc.vector.tensor_copy(pb[t][:], y[t][:].indirect(l2[:]))
-            nc.vector.tensor_copy(pa[t][:], y[t][:].indirect(l1[:]))
-            nc.scalar.activation(size[t][:], pb[t][:], ACT.Abs)
-            nc.scalar.activation(root[t][:], size[t][:], ACT.Abs_reciprocal_sqrt, bias=0.5)
-            nc.scalar.activation(inv[t][:], root[t][:], ACT.Square)
-        for t in range(PACK):
-            nc.vector.tensor_tensor(rb[t][:], pa[t][:], pb[t][:], ALU.max)
-        gb34 = sb([P, PACK], F32, "gb34")
-        nc.scalar.activation(gb34[:], gb_sb[:], ACT.Copy, scale=0.75)
-        for t in range(PACK):
-            nc.scalar.activation(yb[t][:], y[t][:], ACT.Copy, scale=gb34[:, t : t + 1])
-            nc.scalar.activation(yn[t][:], yb[t][:], ACT.Copy, scale=-1.0)
-        for t in range(PACK):
-            nc.vector.tensor_copy(dt[t][:].indirect(l2[:]), rb[t][:])
-        for t in range(PACK):
-            nc.vector.tensor_tensor(dt[t][:].indirect(l1[:]), pa[t][:], inv[t][:], ALU.mult)
-        z_rows = sb([P, PACK, S], BF16, "z_rows")
-        for t in range(PACK):
-            nc.scalar.activation(
-                z_rows[:, t, :].rearrange("p (u m) -> p m u", u=PACK),
-                dt[t][:].rearrange("p (m u) -> p m u", u=PACK),
-                ACT.Copy,
-                scale=ga_sb[:, t : t + 1],
-            )
-        z_bf = held.tile([P, S * PACK], BF16, name="z_bf", tag="z_bf", align_bytes=64)
-        nc.scalar.copy(
-            z_bf[:].rearrange("p (c i t) -> p c t i", i=4, t=PACK),
-            z_rows[:].rearrange("p t (c i) -> p c t i", i=4),
-        )
-        z_codes = sb([P, S], U32, "z_codes")
-        z_scales = sb([P, S], U8, "z_scales")
-        warm = sb([P, 1], F32, "warm")
-        nc.scalar.activation(warm[:], inv[PACK - 1][:, 0:1], ACT.Sigmoid)
+            nc.vector.tensor_tensor(dt[t][:].indirect(l2[:]), pa[:, t, :], lift[:, t, :], ALU.add)
 
-        z2_codes = sb([P, S], U32, "z2_codes")
-        z2_scales = sb([P, S], U8, "z2_scales")
-        s_ps = [bank(PACK + u, f"s_ps{u}") for u in range(PACK)]
-
-        def products(t, c0, c1, first, third, plus, minus):
-            lc = slice(c0 // 16, c1 // 16)
-            nc.vector.tensor_copy(first, yb[t][:].indirect(l3[:, lc]))
-            nc.vector.tensor_copy(third, yn[t][:].indirect(l5[:, lc]))
-            nc.vector.tensor_tensor(plus, y[t][:].indirect(l4[:, lc]), first, ALU.mult)
-            nc.vector.tensor_tensor(minus, y[t][:].indirect(l6[:, lc]), third, ALU.mult)
-
-        def quantise_z2(src, c0, a, b):
-            nc.vector.quantize_mx(
-                out=z2_codes[:, a:b].bitcast(FP8X4),
-                scales=z2_scales[:, a:b],
-                in_=src[:, (a - c0) * PACK : (b - c0) * PACK],
-            )
-
-        def second_product(u, a, b):
-            m = slice(u * P, (u + 1) * P)
-            nc.tensor.matmul_mx(
-                out=s_ps[u][:, a:b],
-                lhsT=z_codes[:, m].bitcast(FP8X4),
-                lhsT_scale=z_scales[:, m],
-                rhs=z2_codes[:, a:b].bitcast(FP8X4),
-                rhs_scale=z2_scales[:, a:b],
-                start=True,
-                stop=True,
-            )
-
-        A = 384
-        first = sb([P, PACK, A], F32, "first")
-        third = sb([P, PACK, A], F32, "third")
-        plus = sb([P, PACK, A], F32, "plus")
-        minus = sb([P, PACK, A], F32, "minus")
-        turned = [bank(b, f"turned{b}") for b in range(A // P)]
+        size = [sb([P, S], F32, f"size{t}") for t in range(PACK)]
+        logs = [sb([P, S], F32, f"logs{t}") for t in range(PACK)]
         for t in range(PACK):
-            products(t, 0, A, first[:, t, :], third[:, t, :], plus[:, t, :], minus[:, t, :])
-            for b in range(A // P):
-                for i, term in enumerate((plus, minus)):
+            nc.scalar.activation(size[t][:], rows[t][:, :S], ACT.Abs)
+        for t in range(PACK):
+            nc.scalar.activation(logs[t][:], size[t][:], ACT.Ln, bias=0.5)
+        inv = sb([P, PACK, W], F32, "inv", tag=f"size{PACK - 1}")
+        for t in range(PACK):
+            nc.scalar.activation(inv[:, t, :], logs[t][:].indirect(l2[:]), ACT.Exp, scale=-1.0)
+        warm_sigmoid = sb([P, 1], F32, "warm_sigmoid")
+        nc.scalar.activation(warm_sigmoid[:], inv[:, PACK - 1, 0:1], ACT.Sigmoid)
+
+        first = sb([P, PACK, S], F32, "first")
+        third = sb([P, PACK, S], F32, "third")
+        plus = sb([P, PACK, S], F32, "plus")
+        minus = sb([P, PACK, S], F32, "minus")
+        turned = [bank(b, f"turned{b}") for b in range(PACK)]
+        for t in range(PACK):
+            nc.vector.tensor_copy(first[:, t, :], yb[t][:].indirect(l3[:]))
+            nc.vector.tensor_scalar(third[:, t, :], yb[t][:].indirect(l5[:]), -1.0, 0.0, ALU.mult, ALU.add)
+            nc.vector.tensor_tensor(plus[:, t, :], rows[t][:].indirect(l4[:]), first[:, t, :], ALU.mult)
+            nc.vector.tensor_tensor(minus[:, t, :], rows[t][:].indirect(l6[:]), third[:, t, :], ALU.mult)
+            for i, term in enumerate((plus, minus)):
+                for b in range(PACK):
                     nc.tensor.matmul(
                         turned[b][:, t * P : (t + 1) * P],
                         term[:, t, b * P : (b + 1) * P],
@@ -201,72 +165,98 @@ def tile_picked_selfratiodetlerp_none_p_kernel(
                         stop=(i == 1),
                         is_transpose=True,
                     )
-        z2_bf = held.tile([P, A * PACK], BF16, name="z2_bf", tag="z2_bf", align_bytes=64)
-        for b in range(A // P):
-            z2_t = sb([P, S], BF16, f"z2_t{b}")
+        z2_bf = sb([P, S * PACK], BF16, "z2_bf")
+        for b in range(PACK):
+            z2_turned = sb([P, S], BF16, f"z2_turned{b}")[:]
             nc.scalar.copy(
-                z2_t[:].rearrange("j (v p e) -> j v p e", v=2, e=2),
+                z2_turned.rearrange("j (v p e) -> j v p e", v=2, e=2),
                 turned[b][:].rearrange("j (v e p) -> j v p e", v=2, e=2),
             )
-            back = bank(3 if b < 2 else 0, f"back{b}")
+            back = bank(PACK + b, f"back{b}")
             for v in range(2):
-                nc.tensor.transpose(back[:, v * P : (v + 1) * P], z2_t[:].bitcast(F32)[:, v * P : (v + 1) * P], ident[:])
+                nc.tensor.transpose(back[:, v * P : (v + 1) * P], z2_turned.bitcast(F32)[:, v * P : (v + 1) * P], ident[:])
             nc.scalar.copy(
                 z2_bf[:].bitcast(F32)[:, 2 * b * P : 2 * (b + 1) * P].rearrange("p (j v) -> p j v", v=2),
                 back[:, : 2 * P].rearrange("p (v j) -> p j v", v=2),
             )
-        nc.vector.quantize_mx(out=z_codes[:].bitcast(FP8X4), scales=z_scales[:], in_=z_bf[:])
-        for a, b in ((0, 256), (256, A)):
-            quantise_z2(z2_bf, 0, a, b)
-        for u in range(PACK):
-            for a, b in ((0, 256), (256, A)):
-                second_product(u, a, b)
-            nc.scalar.activation(s[u][:, :A], s_ps[u][:, :A], ACT.Copy, scale=0.0625)
 
-        n = S - A
-        third2 = sb([P, PACK, n], F32, "third2")
-        plus2 = sb([P, PACK, n], F32, "plus2")
-        minus2 = sb([P, PACK, n], F32, "minus2")
+        z_rows0 = sb([P, PACK, P], BF16, "z_rows0", tag=f"z2_turned{PACK - 1}")
+        z_rows = sb([P, PACK, S - P], BF16, "z_rows", tag=f"z2_turned{PACK - 2}")
         for t in range(PACK):
-            tag = {0: "z_bf", PACK - 1: "z2_bf"}.get(t, f"first2{t}")
-            first2 = held.tile([P, n], F32, name=f"first2{t}", tag=tag, align_bytes=64)
-            products(t, A, S, first2[:], third2[:, t, :], plus2[:, t, :], minus2[:, t, :])
-        z2_bf2 = sb([P, n * PACK], BF16, "z2_bf2")
-        nc.vector.tensor_tensor(
-            z2_bf2[:].rearrange("p (c i t) -> p c t i", i=4, t=PACK),
-            plus2[:].rearrange("p t (c i) -> p c t i", i=4),
-            minus2[:].rearrange("p t (c i) -> p c t i", i=4),
-            ALU.add,
-        )
-        quantise_z2(z2_bf2, A, A, S)
-        for u in range(PACK):
-            second_product(u, A, S)
+            nc.vector.tensor_tensor(dt[t][:].indirect(l1[:]), pa[:, t, :], inv[:, t, :], ALU.mult)
+            dealt = dt[t][:].rearrange("p (m u) -> p m u", u=PACK)
+            weight = ga_sb[:, t : t + 1]
+            nc.scalar.activation(z_rows0[:, t, :], dealt[:, :, 0], ACT.Copy, scale=weight)
+            nc.scalar.activation(
+                z_rows[:, t, :].rearrange("p (u m) -> p m u", u=PACK - 1), dealt[:, :, 1:], ACT.Copy, scale=weight
+            )
+        z2_codes = sb([P, S], U32, "z2_codes")
+        z2_scales = sb([P, S], U8, "z2_scales")
+        quantise(z2_codes[:], z2_scales[:], z2_bf[:])
+
+        z_codes = sb([P, S], U32, "z_codes")
+        z_scales = sb([P, S], U8, "z_scales")
+
+        def weave(copy, z_bf, src):
+            copy(
+                z_bf.rearrange("p (c i t) -> p c t i", i=4, t=PACK),
+                src.rearrange("p t (c i) -> p c t i", i=4),
+            )
+
+        def second_product(acc, u, a, b):
+            m = slice(u * P, (u + 1) * P)
+            product(acc[:, a:b], z_codes[:, m], z_scales[:, m], z2_codes[:, a:b], z2_scales[:, a:b])
+
+        s_ps = [bank(u, f"s_ps{u}") for u in range(PACK)]
+        s_ps_late = bank(PACK, "s_ps_late")
+        z_bf0 = sb([P, S], BF16, "z_bf0")
+        z_bf1 = sb([P, S], BF16, "z_bf1")
+        z_bf2 = sb([P, 2 * S], BF16, "z_bf2")
+        weave(nc.vector.tensor_copy, z_bf0[:], z_rows0[:])
+        quantise(z_codes[:, :P], z_scales[:, :P], z_bf0[:])
+        second_product(s_ps[0], 0, 0, HALF)
+        second_product(s_ps_late, 0, HALF, S)
+        weave(nc.vector.tensor_copy, z_bf1[:], z_rows[:, :, :P])
+        weave(nc.vector.tensor_copy, z_bf2[:, :S], z_rows[:, :, P : 2 * P])
+        weave(nc.scalar.copy, z_bf2[:, S:], z_rows[:, :, 2 * P :])
+        quantise(z_codes[:, P:HALF], z_scales[:, P:HALF], z_bf1[:])
+        second_product(s_ps[1], 1, 0, S)
+        nc.scalar.activation(rows[0][:, :HALF], s_ps[0][:, :HALF], ACT.Copy, scale=0.0625)
+        nc.vector.tensor_scalar(rows[0][:, HALF:S], s_ps_late[:, HALF:], 0.0625, 0.0, ALU.mult, ALU.add)
+        quantise(z_codes[:, HALF:], z_scales[:, HALF:], z_bf2[:])
+        for u in range(2, PACK):
+            second_product(s_ps[u], u, 0, S)
 
         out_rows = out.rearrange("(p u) j -> p u j", u=PACK)
         gate = [sb([P, S], F32, f"gate{u}") for u in range(PACK)]
-        rest = [sb([P, S], F32, f"rest{u}") for u in range(PACK)]
         kept = [sb([P, S], F32, f"kept{u}") for u in range(PACK)]
         taken = [sb([P, S], F32, f"taken{u}") for u in range(PACK)]
+        diff = sb([P, S], F32, "diff")
+        nc.scalar.activation(gate[0][:], rows[0][:].indirect(l8[:]), ACT.Sigmoid)
+        nc.vector.tensor_copy(kept[0][:], rows[0][:].indirect(l7[:]))
+        nc.vector.tensor_tensor(diff[:], rows[0][:].indirect(l9[:]), kept[0][:], ALU.subtract)
+        nc.vector.tensor_tensor(taken[0][:], diff[:], gate[0][:], ALU.mult)
+        A = 384
         last = sb([P, S], F32, "last")
-        for u in range(PACK):
-            nc.scalar.activation(s[u][:, 384:512], s_ps[u][:, 384:512], ACT.Copy, scale=0.0625)
-            parts = ((0, 256), (256, 512)) if u in (0, PACK - 1) else ((0, 512),)
-            for a, b in parts:
-                nc.scalar.activation(gate[u][:, a:b], s[u][:].indirect(l8[:, a // 16 : b // 16]), ACT.Sigmoid)
-                nc.scalar.activation(rest[u][:, a:b], gate[u][:, a:b], ACT.Identity, scale=-1.0, bias=1.0)
-            for a, b in parts:
+        for u in range(1, PACK):
+            rest = sb([P, S], F32, f"rest{u}")
+            nc.scalar.activation(rows[u][:, :S], s_ps[u][:], ACT.Copy, scale=0.0625)
+            nc.scalar.activation(gate[u][:], rows[u][:].indirect(l8[:]), ACT.Sigmoid)
+            nc.scalar.activation(rest[:], gate[u][:], ACT.Identity, scale=-1.0, bias=1.0)
+            for a, b in ((0, A), (A, S)) if u == PACK - 1 else ((0, S),):
                 nc.vector.tensor_tensor(
-                    taken[u][:, a:b], s[u][:].indirect(l9[:, a // 16 : b // 16]), gate[u][:, a:b], ALU.mult
+                    taken[u][:, a:b], rows[u][:].indirect(entries(l9, a, b)), gate[u][:, a:b], ALU.mult
                 )
-                if u > 0 and b == S:
-                    nc.vector.tensor_tensor(gate[u][:], taken[u - 1][:], kept[u - 1][:], ALU.add)
-                    nc.sync.dma_start(out_rows[:, u - 1, :], gate[u][:])
-                if u == PACK - 1 and a > 0:
+                if a == 0:
+                    done = gate[u] if b == S else gate[u - 1]
+                    nc.vector.tensor_tensor(done[:], taken[u - 1][:], kept[u - 1][:], ALU.add)
+                    nc.sync.dma_start(out_rows[:, u - 1, :], done[:])
+                else:
                     nc.vector.tensor_tensor(last[:, :a], taken[u][:, :a], kept[u][:, :a], ALU.add)
                     nc.sync.dma_start(out_rows[:, u, :a], last[:, :a])
                 nc.vector.tensor_tensor(
-                    kept[u][:, a:b], s[u][:].indirect(l7[:, a // 16 : b // 16]), rest[u][:, a:b], ALU.mult
+                    kept[u][:, a:b], rows[u][:].indirect(entries(l7, a, b)), rest[:, a:b], ALU.mult
                 )
         u = PACK - 1
-        nc.vector.tensor_tensor(last[:, HALF:], taken[u][:, HALF:], kept[u][:, HALF:], ALU.add)
-        nc.sync.dma_start(out_rows[:, u, HALF:], last[:, HALF:])
+        nc.vector.tensor_tensor(last[:, A:], taken[u][:, A:], kept[u][:, A:], ALU.add)
+        nc.sync.dma_start(out_rows[:, u, A:], last[:, A:])

@@ -7,6 +7,7 @@ K, T, S, H, W = 512, 2048, 512, 512, 256
 P = 128
 PACK = 4
 HALF = S // 2
+LAST_CUT = 384
 
 F32 = mybir.dt.float32
 BF16 = mybir.dt.bfloat16
@@ -29,8 +30,8 @@ def tile_picked_selfratiodetlerp_none_p_kernel(
         held = ctx.enter_context(tc.tile_pool(name="held", bufs=1))
         psum = ctx.enter_context(tc.psum_pool(name="psum", bufs=1))
 
-        def sb(shape, dtype, name, tag=None):
-            return held.tile(shape, dtype, name=name, tag=tag or name, align_bytes=64)
+        def sb(shape, dtype, name, after=None):
+            return held.tile(shape, dtype, name=name, tag=after or name, align_bytes=64)
 
         def bank(b, name):
             return psum.tile([P, S], F32, name=name, tag=f"bank{b}")
@@ -57,6 +58,9 @@ def tile_picked_selfratiodetlerp_none_p_kernel(
                 stop=True,
             )
 
+        def turn(acc, term, start, stop):
+            nc.tensor.matmul(acc, term, ident[:], start=start, stop=stop, is_transpose=True)
+
         xs_table = sb([P, T], U8, "xs_table")
         nc.gpsimd.memset(xs_table[:].bitcast(I32), 0)
         picks = load_list(offs, "picks")
@@ -80,8 +84,6 @@ def tile_picked_selfratiodetlerp_none_p_kernel(
         yb = [sb([P, 2 * S], F32, f"yb{t}") for t in range(PACK)]
         for t in range(PACK):
             nc.vector.memset(rows[t][:, S:], 0.0)
-        warm_ln = sb([P, 1], F32, "warm_ln")
-        nc.scalar.activation(warm_ln[:], rows[0][:, S : S + 1], ACT.Ln, bias=0.5)
         ident = sb([P, P], F32, "ident")
         make_identity(nc, ident[:])
         for t in range(PACK):
@@ -96,24 +98,24 @@ def tile_picked_selfratiodetlerp_none_p_kernel(
         w_src = w_raw[:].rearrange("p j (m t) -> p m j t", t=PACK)
         nc.vector.tensor_copy(w_dst[:, : P // 2], w_src[:, : P // 2])
         nc.scalar.copy(w_dst[:, P // 2 :], w_src[:, P // 2 :])
-        w_codes = sb([P, H], U32, "w_codes", tag="xs_table")
+        w_codes = sb([P, H], U32, "w_codes", after="xs_table")
         w_scales = sb([P, H], U8, "w_scales")
         quantise(w_codes[:], w_scales[:], w_bf[:])
-        xq_codes = sb([P, S], U32, "xq_codes", tag="w_bf")
+        xq_codes = sb([P, S], U32, "xq_codes", after="w_bf")
         for a in (0, HALF):
             nc.vector.tensor_copy(
                 xq_codes[:, a : a + HALF], x_table[:].bitcast(U32).indirect(entries(picks, a, a + HALF))
             )
         y_ps = [bank(t, f"y_ps{t}") for t in range(PACK)]
-        y_ps_late = bank(PACK, "y_ps_late")
+        y_ps_upper = bank(PACK, "y_ps_upper")
         for t in range(PACK):
             m = slice(t * P, (t + 1) * P)
             for a in (0, HALF):
                 cols = slice(a, a + HALF)
-                acc = y_ps_late if (t, a) == (0, HALF) else y_ps[t]
+                acc = y_ps_upper if (t, a) == (0, HALF) else y_ps[t]
                 product(acc[:, cols], w_codes[:, m], w_scales[:, m], xq_codes[:, cols], xq_scales[:, cols])
         nc.scalar.copy(rows[0][:, :HALF], y_ps[0][:, :HALF])
-        nc.vector.tensor_copy(rows[0][:, HALF:S], y_ps_late[:, HALF:])
+        nc.vector.tensor_copy(rows[0][:, HALF:S], y_ps_upper[:, HALF:])
         for t in range(1, PACK):
             nc.scalar.copy(rows[t][:, :S], y_ps[t][:])
 
@@ -138,12 +140,12 @@ def tile_picked_selfratiodetlerp_none_p_kernel(
         for t in range(PACK):
             nc.scalar.activation(size[t][:], rows[t][:, :S], ACT.Abs)
         for t in range(PACK):
-            nc.scalar.activation(logs[t][:], size[t][:], ACT.Ln, bias=0.5)
-        inv = sb([P, PACK, W], F32, "inv", tag=f"size{PACK - 1}")
+            nc.scalar.activation(logs[t][:], size[t][:], ACT.Ln, scale=2.0, bias=2.0**-60)
+        half_inv = sb([P, PACK, W], F32, "half_inv", after=f"size{PACK - 1}")
+        inv = sb([P, PACK, W], F32, "inv")
         for t in range(PACK):
-            nc.scalar.activation(inv[:, t, :], logs[t][:].indirect(l2[:]), ACT.Exp, scale=-1.0)
-        warm_sigmoid = sb([P, 1], F32, "warm_sigmoid")
-        nc.scalar.activation(warm_sigmoid[:], inv[:, PACK - 1, 0:1], ACT.Sigmoid)
+            nc.scalar.activation(half_inv[:, t, :], logs[t][:].indirect(l2[:]), ACT.Sigmoid, scale=-1.0)
+            nc.scalar.activation(inv[:, t, :], half_inv[:, t, :], ACT.Copy, scale=2.0)
 
         first = sb([P, PACK, S], F32, "first")
         third = sb([P, PACK, S], F32, "third")
@@ -157,31 +159,25 @@ def tile_picked_selfratiodetlerp_none_p_kernel(
             nc.vector.tensor_tensor(minus[:, t, :], rows[t][:].indirect(l6[:]), third[:, t, :], ALU.mult)
             for i, term in enumerate((plus, minus)):
                 for b in range(PACK):
-                    nc.tensor.matmul(
-                        turned[b][:, t * P : (t + 1) * P],
-                        term[:, t, b * P : (b + 1) * P],
-                        ident[:],
-                        start=(i == 0),
-                        stop=(i == 1),
-                        is_transpose=True,
-                    )
+                    turn(turned[b][:, t * P : (t + 1) * P], term[:, t, b * P : (b + 1) * P], i == 0, i == 1)
         z2_bf = sb([P, S * PACK], BF16, "z2_bf")
         for b in range(PACK):
-            z2_turned = sb([P, S], BF16, f"z2_turned{b}")[:]
+            z2_turned = sb([P, S], BF16, f"z2_turned{b}", after=f"logs{b}")
             nc.scalar.copy(
-                z2_turned.rearrange("j (v p e) -> j v p e", v=2, e=2),
+                z2_turned[:].rearrange("j (v p e) -> j v p e", v=2, e=2),
                 turned[b][:].rearrange("j (v e p) -> j v p e", v=2, e=2),
             )
             back = bank(PACK + b, f"back{b}")
             for v in range(2):
-                nc.tensor.transpose(back[:, v * P : (v + 1) * P], z2_turned.bitcast(F32)[:, v * P : (v + 1) * P], ident[:])
+                words = slice(v * P, (v + 1) * P)
+                nc.tensor.transpose(back[:, words], z2_turned[:].bitcast(F32)[:, words], ident[:])
             nc.scalar.copy(
                 z2_bf[:].bitcast(F32)[:, 2 * b * P : 2 * (b + 1) * P].rearrange("p (j v) -> p j v", v=2),
                 back[:, : 2 * P].rearrange("p (v j) -> p j v", v=2),
             )
 
-        z_rows0 = sb([P, PACK, P], BF16, "z_rows0", tag=f"z2_turned{PACK - 1}")
-        z_rows = sb([P, PACK, S - P], BF16, "z_rows", tag=f"z2_turned{PACK - 2}")
+        z_rows0 = sb([P, PACK, P], BF16, "z_rows0", after=f"logs{PACK - 1}")
+        z_rows = sb([P, PACK, S - P], BF16, "z_rows", after=f"logs{PACK - 2}")
         for t in range(PACK):
             nc.vector.tensor_tensor(dt[t][:].indirect(l1[:]), pa[:, t, :], inv[:, t, :], ALU.mult)
             dealt = dt[t][:].rearrange("p (m u) -> p m u", u=PACK)
@@ -208,55 +204,82 @@ def tile_picked_selfratiodetlerp_none_p_kernel(
             product(acc[:, a:b], z_codes[:, m], z_scales[:, m], z2_codes[:, a:b], z2_scales[:, a:b])
 
         s_ps = [bank(u, f"s_ps{u}") for u in range(PACK)]
-        s_ps_late = bank(PACK, "s_ps_late")
+        s_ps_upper = bank(PACK, "s_ps_upper")
         z_bf0 = sb([P, S], BF16, "z_bf0")
         z_bf1 = sb([P, S], BF16, "z_bf1")
-        z_bf2 = sb([P, 2 * S], BF16, "z_bf2")
+        z_bf23 = sb([P, 2 * S], BF16, "z_bf23")
         weave(nc.vector.tensor_copy, z_bf0[:], z_rows0[:])
         quantise(z_codes[:, :P], z_scales[:, :P], z_bf0[:])
         second_product(s_ps[0], 0, 0, HALF)
-        second_product(s_ps_late, 0, HALF, S)
+        second_product(s_ps_upper, 0, HALF, S)
         weave(nc.vector.tensor_copy, z_bf1[:], z_rows[:, :, :P])
-        weave(nc.vector.tensor_copy, z_bf2[:, :S], z_rows[:, :, P : 2 * P])
-        weave(nc.scalar.copy, z_bf2[:, S:], z_rows[:, :, 2 * P :])
+        weave(nc.vector.tensor_copy, z_bf23[:, :S], z_rows[:, :, P : 2 * P])
+        weave(nc.scalar.copy, z_bf23[:, S:], z_rows[:, :, 2 * P :])
         quantise(z_codes[:, P:HALF], z_scales[:, P:HALF], z_bf1[:])
         second_product(s_ps[1], 1, 0, S)
         nc.scalar.activation(rows[0][:, :HALF], s_ps[0][:, :HALF], ACT.Copy, scale=0.0625)
-        nc.vector.tensor_scalar(rows[0][:, HALF:S], s_ps_late[:, HALF:], 0.0625, 0.0, ALU.mult, ALU.add)
-        quantise(z_codes[:, HALF:], z_scales[:, HALF:], z_bf2[:])
+        nc.vector.tensor_scalar(rows[0][:, HALF:S], s_ps_upper[:, HALF:], 0.0625, 0.0, ALU.mult, ALU.add)
+        quantise(z_codes[:, HALF:], z_scales[:, HALF:], z_bf23[:])
         for u in range(2, PACK):
             second_product(s_ps[u], u, 0, S)
 
         out_rows = out.rearrange("(p u) j -> p u j", u=PACK)
         gate = [sb([P, S], F32, f"gate{u}") for u in range(PACK)]
+        rest = [sb([P, S], F32, f"rest{u}") for u in range(PACK)]
         kept = [sb([P, S], F32, f"kept{u}") for u in range(PACK)]
         taken = [sb([P, S], F32, f"taken{u}") for u in range(PACK)]
-        diff = sb([P, S], F32, "diff")
-        nc.scalar.activation(gate[0][:], rows[0][:].indirect(l8[:]), ACT.Sigmoid)
-        nc.vector.tensor_copy(kept[0][:], rows[0][:].indirect(l7[:]))
-        nc.vector.tensor_tensor(diff[:], rows[0][:].indirect(l9[:]), kept[0][:], ALU.subtract)
-        nc.vector.tensor_tensor(taken[0][:], diff[:], gate[0][:], ALU.mult)
-        A = 384
-        last = sb([P, S], F32, "last")
+        done = [sb([P, S], F32, f"done{u}") for u in range(PACK)]
+
+        def look(u, lst, a, b):
+            return rows[u][:].indirect(entries(lst, a, b))
+
+        def gates(u, a, b):
+            nc.scalar.activation(gate[u][:, a:b], look(u, l8, a, b), ACT.Sigmoid)
+            nc.scalar.activation(rest[u][:, a:b], gate[u][:, a:b], ACT.Identity, scale=-1.0, bias=1.0)
+
+        def take(u, a, b):
+            nc.vector.tensor_tensor(taken[u][:, a:b], look(u, l9, a, b), gate[u][:, a:b], ALU.mult)
+
+        def keep(u, a, b):
+            nc.vector.tensor_tensor(kept[u][:, a:b], look(u, l7, a, b), rest[u][:, a:b], ALU.mult)
+
+        def finish(u, a, b):
+            nc.vector.tensor_tensor(done[u][:, a:b], taken[u][:, a:b], kept[u][:, a:b], ALU.add)
+            nc.sync.dma_start(out_rows[:, u, a:b], done[u][:, a:b])
+
+        diff = sb([P, HALF], F32, "diff")
+        gates(0, HALF, S)
+        nc.scalar.activation(gate[0][:, :HALF], look(0, l8, 0, HALF), ACT.Sigmoid)
+        nc.vector.tensor_copy(kept[0][:, :HALF], look(0, l7, 0, HALF))
+        nc.vector.tensor_tensor(diff[:], look(0, l9, 0, HALF), kept[0][:, :HALF], ALU.subtract)
+        take(0, HALF, S)
+        keep(0, HALF, S)
+        nc.vector.tensor_tensor(taken[0][:, :HALF], diff[:], gate[0][:, :HALF], ALU.mult)
+        finish(0, 0, S)
         for u in range(1, PACK):
-            rest = sb([P, S], F32, f"rest{u}")
             nc.scalar.activation(rows[u][:, :S], s_ps[u][:], ACT.Copy, scale=0.0625)
-            nc.scalar.activation(gate[u][:], rows[u][:].indirect(l8[:]), ACT.Sigmoid)
-            nc.scalar.activation(rest[:], gate[u][:], ACT.Identity, scale=-1.0, bias=1.0)
-            for a, b in ((0, A), (A, S)) if u == PACK - 1 else ((0, S),):
-                nc.vector.tensor_tensor(
-                    taken[u][:, a:b], rows[u][:].indirect(entries(l9, a, b)), gate[u][:, a:b], ALU.mult
-                )
-                if a == 0:
-                    done = gate[u] if b == S else gate[u - 1]
-                    nc.vector.tensor_tensor(done[:], taken[u - 1][:], kept[u - 1][:], ALU.add)
-                    nc.sync.dma_start(out_rows[:, u - 1, :], done[:])
-                else:
-                    nc.vector.tensor_tensor(last[:, :a], taken[u][:, :a], kept[u][:, :a], ALU.add)
-                    nc.sync.dma_start(out_rows[:, u, :a], last[:, :a])
-                nc.vector.tensor_tensor(
-                    kept[u][:, a:b], rows[u][:].indirect(entries(l7, a, b)), rest[:, a:b], ALU.mult
-                )
-        u = PACK - 1
-        nc.vector.tensor_tensor(last[:, A:], taken[u][:, A:], kept[u][:, A:], ALU.add)
-        nc.sync.dma_start(out_rows[:, u, A:], last[:, A:])
+            gates(u, 0, S)
+        for u in (1, 2):
+            take(u, 0, S)
+            keep(u, 0, S)
+        take(3, 0, LAST_CUT)
+        finish(2, 0, S)
+        keep(3, 0, LAST_CUT)
+        take(3, LAST_CUT, S)
+        finish(3, 0, LAST_CUT)
+        keep(3, LAST_CUT, S)
+        finish(3, LAST_CUT, S)
+
+        sums = bank(PACK - 1, "sums")
+        for b in range(PACK):
+            cols = slice(b * P, (b + 1) * P)
+            for i, term in enumerate((taken[1], kept[1])):
+                turn(sums[:, cols], term[:, cols], i == 0, i == 1)
+        sums_sb = sb([P, S], F32, "sums_sb")
+        nc.scalar.copy(sums_sb[:], sums[:])
+        sums_back = bank(PACK + 1, "sums_back")
+        for b in range(PACK):
+            cols = slice(b * P, (b + 1) * P)
+            nc.tensor.transpose(sums_back[:, cols], sums_sb[:, cols], ident[:])
+        nc.scalar.copy(done[1][:], sums_back[:])
+        nc.scalar.dma_start(out_rows[:, 1, :], done[1][:])

from contextlib import ExitStack

import concourse.mybir as mybir
from concourse.masks import make_identity

K, T, S, H, W = 512, 2048, 512, 512, 256
P = 128
PACK = 4
HALF = S // 2
LAST_CUT = 384

F32 = mybir.dt.float32
BF16 = mybir.dt.bfloat16
I32 = mybir.dt.int32
U32 = mybir.dt.uint32
U16 = mybir.dt.uint16
U8 = mybir.dt.uint8
FP8X4 = mybir.dt.float8_e4m3fn_x4
ALU = mybir.AluOpType
ACT = mybir.ActivationFunctionType

FLOPS = 2 * K * H * S + 2 * H * S * S


def tile_picked_selfratiodetlerp_none_p_kernel(
    tc, x_words, x_scales, w1, ga, gb, offs, n1, n2, n3, n4, n5, n6, n7, n8, n9, out
):
    nc = tc.nc
    with ExitStack() as ctx:
        held = ctx.enter_context(tc.tile_pool(name="held", bufs=1))
        psum = ctx.enter_context(tc.psum_pool(name="psum", bufs=1))

        def sb(shape, dtype, name, after=None):
            return held.tile(shape, dtype, name=name, tag=after or name, align_bytes=64)

        def bank(b, name):
            return psum.tile([P, S], F32, name=name, tag=f"bank{b}")

        def load_list(src, name):
            lst = sb(list(src.shape), U16, name)
            nc.sync.dma_start(lst[:], src)
            return lst

        def entries(lst, a, b):
            return lst[:, a // 16 : b // 16]

        def quantise(codes, scales, values):
            nc.vector.quantize_mx(out=codes.bitcast(FP8X4), scales=scales, in_=values)

        def product(acc, left, left_scales, right, right_scales):
            nc.tensor.matmul_mx(
                out=acc,
                lhsT=left.bitcast(FP8X4),
                lhsT_scale=left_scales,
                rhs=right.bitcast(FP8X4),
                rhs_scale=right_scales,
                start=True,
                stop=True,
            )

        def turn(acc, term, start, stop):
            nc.tensor.matmul(acc, term, ident[:], start=start, stop=stop, is_transpose=True)

        xs_table = sb([P, T], U8, "xs_table")
        nc.gpsimd.memset(xs_table[:].bitcast(I32), 0)
        picks = load_list(offs, "picks")
        w_raw = sb([P, PACK, H], F32, "w_raw")
        nc.sync.dma_start(w_raw[:], w1.rearrange("(p j) c -> p j c", j=PACK))
        for q in range(4):
            nc.sync.dma_start(
                xs_table[32 * q : 32 * q + 4, :].bitcast(I32), x_scales[0, 4 * q : 4 * q + 4, :].bitcast(I32)
            )
        x_table = sb([P, T], I32, "x_table")
        nc.sync.dma_start(x_table[:], x_words[0].rearrange("p n r -> p (n r)").bitcast(I32))
        l1, l2 = load_list(n1, "l1"), load_list(n2, "l2")
        gb_sb = sb([P, PACK], F32, "gb_sb")
        nc.sync.dma_start(gb_sb[:], gb.rearrange("(p t) o -> p (t o)", t=PACK))
        l3, l5, l4, l6 = load_list(n3, "l3"), load_list(n5, "l5"), load_list(n4, "l4"), load_list(n6, "l6")
        ga_sb = sb([P, PACK], F32, "ga_sb")
        nc.sync.dma_start(ga_sb[:], ga.rearrange("(p t) o -> p (t o)", t=PACK))
        l7, l9, l8 = load_list(n7, "l7"), load_list(n9, "l9"), load_list(n8, "l8")

        rows = [sb([P, 2 * S], F32, f"rows{t}") for t in range(PACK)]
        yb = [sb([P, 2 * S], F32, f"yb{t}") for t in range(PACK)]
        for t in range(PACK):
            nc.vector.memset(rows[t][:, S:], 0.0)
        ident = sb([P, P], F32, "ident")
        make_identity(nc, ident[:])
        for t in range(PACK):
            nc.gpsimd.memset(yb[t][:, S:], 0.0)
        gb34 = sb([P, PACK], F32, "gb34")
        nc.gpsimd.tensor_scalar(gb34[:], gb_sb[:], 0.75, 0.0, ALU.mult, ALU.add)

        xq_scales = sb([P, S], U8, "xq_scales")
        nc.vector.tensor_copy(xq_scales[:], xs_table[:].indirect(picks[:]))
        w_bf = sb([P, H * PACK], BF16, "w_bf")
        w_dst = w_bf[:].rearrange("p (t m j) -> p m j t", t=PACK, j=PACK)
        w_src = w_raw[:].rearrange("p j (m t) -> p m j t", t=PACK)
        nc.vector.tensor_copy(w_dst[:, : P // 2], w_src[:, : P // 2])
        nc.scalar.copy(w_dst[:, P // 2 :], w_src[:, P // 2 :])
        w_codes = sb([P, H], U32, "w_codes", after="xs_table")
        w_scales = sb([P, H], U8, "w_scales")
        quantise(w_codes[:], w_scales[:], w_bf[:])
        xq_codes = sb([P, S], U32, "xq_codes", after="w_bf")
        for a in (0, HALF):
            nc.vector.tensor_copy(
                xq_codes[:, a : a + HALF], x_table[:].bitcast(U32).indirect(entries(picks, a, a + HALF))
            )
        y_ps = [bank(t, f"y_ps{t}") for t in range(PACK)]
        y_ps_upper = bank(PACK, "y_ps_upper")
        for t in range(PACK):
            m = slice(t * P, (t + 1) * P)
            for a in (0, HALF):
                cols = slice(a, a + HALF)
                acc = y_ps_upper if (t, a) == (0, HALF) else y_ps[t]
                product(acc[:, cols], w_codes[:, m], w_scales[:, m], xq_codes[:, cols], xq_scales[:, cols])
        nc.scalar.copy(rows[0][:, :HALF], y_ps[0][:, :HALF])
        nc.vector.tensor_copy(rows[0][:, HALF:S], y_ps_upper[:, HALF:])
        for t in range(1, PACK):
            nc.scalar.copy(rows[t][:, :S], y_ps[t][:])

        pa = sb([P, PACK, W], F32, "pa")
        gap = sb([P, PACK, W], F32, "gap")
        lift = sb([P, PACK, W], F32, "lift")
        dt = [sb([P, S], F32, f"dt{t}") for t in range(PACK)]
        for t0 in range(0, PACK, 2):
            pair = (t0, t0 + 1)
            for t in pair:
                nc.vector.tensor_copy(pa[:, t, :], rows[t][:].indirect(l1[:]))
            for t in pair:
                nc.vector.tensor_tensor(gap[:, t, :], rows[t][:].indirect(l2[:]), pa[:, t, :], ALU.subtract)
            for t in pair:
                nc.scalar.activation(yb[t][:, :S], rows[t][:, :S], ACT.Copy, scale=gb34[:, t : t + 1])
            nc.scalar.activation(lift[:, t0 : t0 + 2, :], gap[:, t0 : t0 + 2, :], ACT.Relu)
        for t in range(PACK):
            nc.vector.tensor_tensor(dt[t][:].indirect(l2[:]), pa[:, t, :], lift[:, t, :], ALU.add)

        size = [sb([P, S], F32, f"size{t}") for t in range(PACK)]
        logs = [sb([P, S], F32, f"logs{t}") for t in range(PACK)]
        for t in range(PACK):
            nc.scalar.activation(size[t][:], rows[t][:, :S], ACT.Abs)
        for t in range(PACK):
            nc.scalar.activation(logs[t][:], size[t][:], ACT.Ln, scale=2.0, bias=2.0**-60)
        half_inv = sb([P, PACK, W], F32, "half_inv", after=f"size{PACK - 1}")
        inv = sb([P, PACK, W], F32, "inv")
        for t in range(PACK):
            nc.scalar.activation(half_inv[:, t, :], logs[t][:].indirect(l2[:]), ACT.Sigmoid, scale=-1.0)
            nc.scalar.activation(inv[:, t, :], half_inv[:, t, :], ACT.Copy, scale=2.0)

        first = sb([P, PACK, S], F32, "first")
        third = sb([P, PACK, S], F32, "third")
        plus = sb([P, PACK, S], F32, "plus")
        minus = sb([P, PACK, S], F32, "minus")
        turned = [bank(b, f"turned{b}") for b in range(PACK)]
        for t in range(PACK):
            nc.vector.tensor_copy(first[:, t, :], yb[t][:].indirect(l3[:]))
            nc.vector.tensor_scalar(third[:, t, :], yb[t][:].indirect(l5[:]), -1.0, 0.0, ALU.mult, ALU.add)
            nc.vector.tensor_tensor(plus[:, t, :], rows[t][:].indirect(l4[:]), first[:, t, :], ALU.mult)
            nc.vector.tensor_tensor(minus[:, t, :], rows[t][:].indirect(l6[:]), third[:, t, :], ALU.mult)
            for i, term in enumerate((plus, minus)):
                for b in range(PACK):
                    turn(turned[b][:, t * P : (t + 1) * P], term[:, t, b * P : (b + 1) * P], i == 0, i == 1)
        z2_bf = sb([P, S * PACK], BF16, "z2_bf")
        for b in range(PACK):
            z2_turned = sb([P, S], BF16, f"z2_turned{b}", after=f"logs{b}")
            nc.scalar.copy(
                z2_turned[:].rearrange("j (v p e) -> j v p e", v=2, e=2),
                turned[b][:].rearrange("j (v e p) -> j v p e", v=2, e=2),
            )
            back = bank(PACK + b, f"back{b}")
            for v in range(2):
                words = slice(v * P, (v + 1) * P)
                nc.tensor.transpose(back[:, words], z2_turned[:].bitcast(F32)[:, words], ident[:])
            nc.scalar.copy(
                z2_bf[:].bitcast(F32)[:, 2 * b * P : 2 * (b + 1) * P].rearrange("p (j v) -> p j v", v=2),
                back[:, : 2 * P].rearrange("p (v j) -> p j v", v=2),
            )

        z_rows0 = sb([P, PACK, P], BF16, "z_rows0", after=f"logs{PACK - 1}")
        z_rows = sb([P, PACK, S - P], BF16, "z_rows", after=f"logs{PACK - 2}")
        for t in range(PACK):
            nc.vector.tensor_tensor(dt[t][:].indirect(l1[:]), pa[:, t, :], inv[:, t, :], ALU.mult)
            dealt = dt[t][:].rearrange("p (m u) -> p m u", u=PACK)
            weight = ga_sb[:, t : t + 1]
            nc.scalar.activation(z_rows0[:, t, :], dealt[:, :, 0], ACT.Copy, scale=weight)
            nc.scalar.activation(
                z_rows[:, t, :].rearrange("p (u m) -> p m u", u=PACK - 1), dealt[:, :, 1:], ACT.Copy, scale=weight
            )
        z2_codes = sb([P, S], U32, "z2_codes")
        z2_scales = sb([P, S], U8, "z2_scales")
        quantise(z2_codes[:], z2_scales[:], z2_bf[:])

        z_codes = sb([P, S], U32, "z_codes")
        z_scales = sb([P, S], U8, "z_scales")

        def weave(copy, z_bf, src):
            copy(
                z_bf.rearrange("p (c i t) -> p c t i", i=4, t=PACK),
                src.rearrange("p t (c i) -> p c t i", i=4),
            )

        def second_product(acc, u, a, b):
            m = slice(u * P, (u + 1) * P)
            product(acc[:, a:b], z_codes[:, m], z_scales[:, m], z2_codes[:, a:b], z2_scales[:, a:b])

        s_ps = [bank(u, f"s_ps{u}") for u in range(PACK)]
        s_ps_upper = bank(PACK, "s_ps_upper")
        z_bf0 = sb([P, S], BF16, "z_bf0")
        z_bf1 = sb([P, S], BF16, "z_bf1")
        z_bf23 = sb([P, 2 * S], BF16, "z_bf23")
        weave(nc.vector.tensor_copy, z_bf0[:], z_rows0[:])
        quantise(z_codes[:, :P], z_scales[:, :P], z_bf0[:])
        second_product(s_ps[0], 0, 0, HALF)
        second_product(s_ps_upper, 0, HALF, S)
        weave(nc.vector.tensor_copy, z_bf1[:], z_rows[:, :, :P])
        weave(nc.vector.tensor_copy, z_bf23[:, :S], z_rows[:, :, P : 2 * P])
        weave(nc.scalar.copy, z_bf23[:, S:], z_rows[:, :, 2 * P :])
        quantise(z_codes[:, P:HALF], z_scales[:, P:HALF], z_bf1[:])
        second_product(s_ps[1], 1, 0, S)
        nc.scalar.activation(rows[0][:, :HALF], s_ps[0][:, :HALF], ACT.Copy, scale=0.0625)
        nc.vector.tensor_scalar(rows[0][:, HALF:S], s_ps_upper[:, HALF:], 0.0625, 0.0, ALU.mult, ALU.add)
        quantise(z_codes[:, HALF:], z_scales[:, HALF:], z_bf23[:])
        for u in range(2, PACK):
            second_product(s_ps[u], u, 0, S)

        out_rows = out.rearrange("(p u) j -> p u j", u=PACK)
        gate = [sb([P, S], F32, f"gate{u}") for u in range(PACK)]
        rest = [sb([P, S], F32, f"rest{u}") for u in range(PACK)]
        kept = [sb([P, S], F32, f"kept{u}") for u in range(PACK)]
        taken = [sb([P, S], F32, f"taken{u}") for u in range(PACK)]
        done = [sb([P, S], F32, f"done{u}") for u in range(PACK)]

        def look(u, lst, a, b):
            return rows[u][:].indirect(entries(lst, a, b))

        def gates(u, a, b):
            nc.scalar.activation(gate[u][:, a:b], look(u, l8, a, b), ACT.Sigmoid)
            nc.scalar.activation(rest[u][:, a:b], gate[u][:, a:b], ACT.Identity, scale=-1.0, bias=1.0)

        def take(u, a, b):
            nc.vector.tensor_tensor(taken[u][:, a:b], look(u, l9, a, b), gate[u][:, a:b], ALU.mult)

        def keep(u, a, b):
            nc.vector.tensor_tensor(kept[u][:, a:b], look(u, l7, a, b), rest[u][:, a:b], ALU.mult)

        def finish(u, a, b):
            nc.vector.tensor_tensor(done[u][:, a:b], taken[u][:, a:b], kept[u][:, a:b], ALU.add)
            nc.sync.dma_start(out_rows[:, u, a:b], done[u][:, a:b])

        diff = sb([P, HALF], F32, "diff")
        gates(0, HALF, S)
        nc.scalar.activation(gate[0][:, :HALF], look(0, l8, 0, HALF), ACT.Sigmoid)
        nc.vector.tensor_copy(kept[0][:, :HALF], look(0, l7, 0, HALF))
        nc.vector.tensor_tensor(diff[:], look(0, l9, 0, HALF), kept[0][:, :HALF], ALU.subtract)
        take(0, HALF, S)
        keep(0, HALF, S)
        nc.vector.tensor_tensor(taken[0][:, :HALF], diff[:], gate[0][:, :HALF], ALU.mult)
        finish(0, 0, S)
        for u in range(1, PACK):
            nc.scalar.activation(rows[u][:, :S], s_ps[u][:], ACT.Copy, scale=0.0625)
            gates(u, 0, S)
        for u in (1, 2):
            take(u, 0, S)
            keep(u, 0, S)
        take(3, 0, LAST_CUT)
        finish(2, 0, S)
        keep(3, 0, LAST_CUT)
        take(3, LAST_CUT, S)
        finish(3, 0, LAST_CUT)
        keep(3, LAST_CUT, S)
        finish(3, LAST_CUT, S)

        sums = bank(PACK - 1, "sums")
        for b in range(PACK):
            cols = slice(b * P, (b + 1) * P)
            for i, term in enumerate((taken[1], kept[1])):
                turn(sums[:, cols], term[:, cols], i == 0, i == 1)
        sums_sb = sb([P, S], F32, "sums_sb")
        nc.scalar.copy(sums_sb[:], sums[:])
        sums_back = bank(PACK + 1, "sums_back")
        for b in range(PACK):
            cols = slice(b * P, (b + 1) * P)
            nc.tensor.transpose(sums_back[:, cols], sums_sb[:, cols], ident[:])
        nc.scalar.copy(done[1][:], sums_back[:])
        nc.scalar.dma_start(out_rows[:, 1, :], done[1][:])
